import numpy as np
import ml_dtypes


def mxq(x, axis, fmt="e4m3"):
    dtype, down = {"e4m3": (ml_dtypes.float8_e4m3fn, 7), "e5m2": (ml_dtypes.float8_e5m2, 14)}[fmt]
    v = np.moveaxis(np.asarray(x, np.float32).astype(ml_dtypes.bfloat16).astype(np.float64), axis, -1)
    blocks = v.reshape(v.shape[:-1] + (-1, 32))
    amax = np.abs(blocks).max(-1, keepdims=True)
    byte = np.maximum(np.where(amax > 0, np.frexp(amax)[1] - 1 + 127, 0) - down, 1)
    scale = np.exp2(byte - 127.0)
    codes = (blocks / scale).astype(np.float32).astype(dtype).astype(np.float64)
    return np.moveaxis((codes * scale).reshape(v.shape), -1, axis)


WIDE = False


def mx_kscale(k):
    if not WIDE:
        return np.ones(k)
    levels = np.array([30, -30])
    if k % 512:
        return np.exp2(np.random.permutation(np.resize(levels, k // 32))).repeat(32)
    a = np.empty((k // 512, 16))
    for p in range(k // 512):
        a[p, :8] = np.random.permutation(np.resize(levels, 8))
        for g in range(8):
            far = levels[np.abs(levels - a[p, g]) >= 10]
            a[p, g + 8] = far[np.random.randint(len(far))]
    return np.exp2(a.ravel()).repeat(32)


def f64(x):
    return np.asarray(x).astype(np.float64)


E2M1 = np.array([0.0, 0.5, 1.0, 1.5, 2.0, 3.0, 4.0, 6.0, -0.0, -0.5, -1.0, -1.5, -2.0, -3.0, -4.0, -6.0])


def pack_weight(w, fmt):
    k, n = w.shape
    w = f64(np.asarray(w, np.float32).astype(ml_dtypes.bfloat16)).reshape(k // 32, 32, n)
    amax = np.abs(w).max(1)
    if fmt == "e4m3":
        byte = np.frexp(amax)[1] - 1 + 127 - 7
    else:
        mant, ex = np.frexp(amax / 6.0)
        byte = np.where(mant > 0.5, ex, ex - 1) + 127
    byte = np.clip(np.where(amax > 0, byte, 1), 1, 254)
    scaled = (w * np.exp2(127.0 - byte)[:, None, :]).reshape(k, n).astype(np.float32)
    by_word = np.ascontiguousarray(scaled.reshape(k // 512, 128, 4, n).transpose(0, 1, 3, 2))
    if fmt == "e4m3":
        words = by_word.astype(ml_dtypes.float8_e4m3fn).view(np.uint8)
    else:
        c = by_word.astype(ml_dtypes.float4_e2m1fn).view(np.uint8) & 0xF
        words = (c[..., 0::2] | (c[..., 1::2] << 4)).reshape(k // 512, 128, 2 * n)
    return np.ascontiguousarray(words), np.ascontiguousarray(byte.astype(np.uint8).reshape(k // 512, 16, n))


def unpack_weight(words, scales, fmt):
    g, _, n = scales.shape
    words = np.ascontiguousarray(words).reshape(g, 128, n, -1)
    if fmt == "e4m3":
        vals = words.view(ml_dtypes.float8_e4m3fn).astype(np.float64)
    else:
        nib = np.empty((g, 128, n, 4), np.uint8)
        nib[..., 0::2] = words & 0xF
        nib[..., 1::2] = words >> 4
        vals = E2M1[nib]
    vals = vals * np.repeat(np.exp2(scales.astype(np.float64) - 127.0), 8, axis=1)[..., None]
    return vals.transpose(0, 1, 3, 2).reshape(g * 512, n)


def bf(x):
    return np.asarray(x, np.float32).astype(ml_dtypes.bfloat16)


def planes(Y):
    r, m = Y.shape
    b = f64(bf(Y)).reshape(r // 32, 32, m)
    amax = np.abs(b).max(1)
    byte = np.clip(np.where(amax > 0, np.frexp(amax)[1] - 1 + 127 - 7, 1), 1, 254)
    codes = (b * np.exp2(127.0 - byte)[:, None, :]).reshape(r, m).astype(np.float32).astype(ml_dtypes.float8_e4m3fn).view(np.uint8)
    words = codes.reshape(r // 512, 128, 4, m).transpose(0, 1, 3, 2)
    return np.ascontiguousarray(words), np.ascontiguousarray(byte.astype(np.uint8).reshape(r // 512, 16, m))


N, L, R, K, T, B = 512, 1024, 512, 512, 512, 128


def setup_inputs():
    n = np.random.standard_normal
    fn = mx_kscale(N)
    fl = mx_kscale(L)
    fr = mx_kscale(R)
    wdp = pack_weight(n((N, R)) * 1 / np.sqrt(N) * fn[:, None], "e4m3")
    xqp = pack_weight(n((L, T)) / fl[:, None], "e2m1")
    wsp = pack_weight(n((L, R)) * 1 / np.sqrt(L) * fl[:, None], "e4m3")
    wup = pack_weight(n((R, K)) * 1 / np.sqrt(R) / fr[:, None], "e2m1")
    return {
        "g": (n((N, T)) * np.exp(0.5 * n((1, T))) / fn[:, None]).astype(np.float32),
        "wd_words": wdp[0],
        "wd_scales": wdp[1],
        "xq_words": xqp[0],
        "xq_scales": xqp[1],
        "ws_words": wsp[0],
        "ws_scales": wsp[1],
        "us": (np.random.uniform(0.5, 2.0, (R, 1)) * fr[:, None]).astype(np.float32),
        "wu_words": wup[0],
        "wu_scales": wup[1],
    }


def reference(g, wd_words, wd_scales, xq_words, xq_scales, ws_words, ws_scales, us, wu_words, wu_scales):
    wdu = unpack_weight(wd_words, wd_scales, "e4m3")
    xqu = unpack_weight(xq_words, xq_scales, "e2m1")
    wsu = unpack_weight(ws_words, ws_scales, "e4m3")
    wuu = unpack_weight(wu_words, wu_scales, "e2m1")
    gq = mxq(f64(g), 0, "e5m2")
    d = wdu.T @ gq + wsu.T @ xqu
    m = d.reshape(R, B, T // B).mean(axis=2)
    mr = np.repeat(m, T // B, axis=1)
    dz = (0.5 * d + 0.5 * mr) * f64(us)
    dzq = mxq(dz, 0, "e5m2")
    y = wuu.T @ dzq
    words, scales = planes(y)
    return y, words, scales

@@ -1,0 +1,225 @@
+from contextlib import ExitStack
+
+import concourse.mybir as mybir
+
+N, L, R, K, T = 512, 1024, 512, 512, 512
+FLOPS = 2 * T * (N * R + L * R + R * K)
+
+F32 = mybir.dt.float32
+BF16 = mybir.dt.bfloat16
+I32 = mybir.dt.int32
+U8 = mybir.dt.uint8
+E4M3 = mybir.dt.float8_e4m3fn_x4
+E5M2 = mybir.dt.float8_e5m2_x4
+E2M1 = mybir.dt.float4_e2m1fn_x4
+ALU = mybir.AluOpType
+ACT = mybir.ActivationFunctionType
+AXIS = mybir.AxisListType
+
+P = 128
+PACK = 4
+GROUP = 4
+HALF = T // 2
+G_VECTOR = 168
+Y_VECTOR = 336
+WARM = 0
+
+
+def load_scale_rows(queue, plane, scales, quadrant):
+    queue.dma_start(
+        out=plane[32 * quadrant : 32 * quadrant + 4, :, :].bitcast(I32),
+        in_=scales[:, 4 * quadrant : 4 * quadrant + 4, :].rearrange("z r c -> r z c").bitcast(I32),
+    )
+
+
+def deal_words(nc, dealt, raw):
+    nc.vector.tensor_copy(
+        out=dealt.rearrange("p (j c i) -> p c j i", j=PACK, i=4),
+        in_=raw.rearrange("p (c i j) -> p c j i", j=PACK, i=4),
+    )
+
+
+def deal_scales(nc, dealt, raw):
+    nc.vector.tensor_copy(
+        out=dealt.rearrange("p z (j m) -> p z j m", j=PACK),
+        in_=raw.rearrange("p z (m j) -> p z j m", j=PACK),
+    )
+
+
+def interleave(copy, grouped, rows, first, last):
+    copy(
+        out=grouped[:, PACK * first : PACK * last].rearrange("p (c i j) -> p c j i", i=4, j=PACK),
+        in_=rows[:, :, first:last].rearrange("p j (c i) -> p c j i", i=4),
+    )
+
+
+def tile_mix_gradient_shared_by_neighbours_pl_kernel(
+    tc, g, wd_words, wd_scales, xq_words, xq_scales, ws_words, ws_scales, us, wu_words, wu_scales, out_0, out_1, out_2
+):
+    nc = tc.nc
+    with ExitStack() as ctx:
+        sb = ctx.enter_context(tc.tile_pool(name="sb", bufs=1))
+        ps = ctx.enter_context(tc.psum_pool(name="ps", bufs=1))
+        ctx.enter_context(tc.manual_schedule())
+
+        ws_plane_raw = sb.tile([P, 2, R], U8, align_bytes=64)
+        xq_plane = sb.tile([P, 2, T], U8, align_bytes=64)
+        wd_plane_raw = sb.tile([P, 1, R], U8, align_bytes=64)
+        wu_plane_raw = sb.tile([P, 1, K], U8, align_bytes=64)
+        ws_plane = sb.tile([P, 2, R], U8, align_bytes=64)
+        wd_plane = sb.tile([P, 1, R], U8, align_bytes=64)
+        wu_plane = sb.tile([P, 1, K], U8, align_bytes=64)
+        ws_raw = [sb.tile([P, R], I32, name="ws_raw%d" % z, align_bytes=64) for z in range(2)]
+        ws_codes = [sb.tile([P, R], I32, name="ws_codes%d" % z, align_bytes=64) for z in range(2)]
+        wd_raw = sb.tile([P, R], I32, align_bytes=64)
+        wd_codes = sb.tile([P, R], I32, align_bytes=64)
+        xq_codes = sb.tile([P, 2, 2 * T], U8, align_bytes=64)
+        wu_raw = sb.tile([P, 2 * K], U8, align_bytes=64)
+        wu_codes = sb.tile([P, 2 * K], U8, align_bytes=64)
+        g_raw = [sb.tile([P, PACK, HALF], F32, name="g_raw%d" % h, align_bytes=64) for h in range(2)]
+        g_bf = [sb.tile([P, PACK * HALF], BF16, name="g_bf%d" % h, align_bytes=64) for h in range(2)]
+        g_codes = sb.tile([P, T], I32, align_bytes=64)
+        g_plane = sb.tile([P, T], U8, align_bytes=64)
+        us_raw = sb.tile([P, PACK], F32, align_bytes=64)
+        us_half = sb.tile([P, PACK], F32, align_bytes=64)
+        us_eighth = sb.tile([P, PACK], F32, align_bytes=64)
+        warm = sb.tile([P, 1], F32, align_bytes=64)
+        warm_out = sb.tile([P, 1], F32, align_bytes=64)
+
+        nc.gpsimd.memset(ws_plane_raw[:].bitcast(I32), 0)
+        for plane in (xq_plane, wd_plane_raw, wu_plane_raw):
+            nc.vector.memset(plane[:].bitcast(I32), 0)
+        nc.vector.memset(warm[:], 0.0)
+        nc.scalar.activation(out=warm_out[:], in_=warm[:], func=ACT.Copy)
+
+        g_rows = g.rearrange("(p j) t -> p j t", j=PACK)
+        nc.sync.dma_start(out=ws_raw[0][:], in_=ws_words[0].rearrange("p c t -> p (c t)").bitcast(I32))
+        for q in range(4):
+            load_scale_rows(nc.sync, ws_plane_raw, ws_scales, q)
+        for q in range(2):
+            load_scale_rows(nc.sync, xq_plane, xq_scales, q)
+        nc.sync.dma_start(out=xq_codes[:].bitcast(I32), in_=xq_words.rearrange("z p c -> p z c").bitcast(I32))
+        for q in range(2, 4):
+            load_scale_rows(nc.sync, xq_plane, xq_scales, q)
+        nc.sync.dma_start(out=ws_raw[1][:], in_=ws_words[1].rearrange("p c t -> p (c t)").bitcast(I32))
+        nc.sync.dma_start(out=g_raw[0][:], in_=g_rows[:, :, 0:HALF])
+        for q in range(4):
+            load_scale_rows(nc.sync, wd_plane_raw, wd_scales, q)
+        nc.sync.dma_start(out=g_raw[1][:], in_=g_rows[:, :, HALF:T])
+        nc.sync.dma_start(out=wd_raw[:], in_=wd_words[0].rearrange("p c t -> p (c t)").bitcast(I32))
+        nc.sync.dma_start(out=wu_raw[:].bitcast(I32), in_=wu_words[0].bitcast(I32))
+        nc.sync.dma_start(out=us_raw[:], in_=us.rearrange("(p j) o -> p (j o)", j=PACK))
+        for q in range(4):
+            load_scale_rows(nc.sync, wu_plane_raw, wu_scales, q)
+
+        d_banks = [ps.tile([P, T], F32, name="d_bank%d" % j, tag="d%d" % j) for j in range(PACK)]
+
+        def first_pass(j, codes, plane, moving, moving_plane, start, stop):
+            cols = slice(j * P, (j + 1) * P)
+            nc.tensor.matmul_mx(
+                out=d_banks[j][:], lhsT=codes[:, cols].bitcast(E4M3), lhsT_scale=plane[:, cols],
+                rhs=moving, rhs_scale=moving_plane, start=start, stop=stop,
+            )
+
+        deal_scales(nc, ws_plane[:], ws_plane_raw[:])
+        for z in range(2):
+            deal_words(nc, ws_codes[z][:], ws_raw[z][:])
+            for j in range(PACK):
+                first_pass(j, ws_codes[z], ws_plane[:, z, :], xq_codes[:, z, :].bitcast(E2M1), xq_plane[:, z, :], z == 0, False)
+        deal_scales(nc, wd_plane[:], wd_plane_raw[:])
+
+        def quantise(fmt, codes, plane, grouped, first, last):
+            nc.vector.quantize_mx(out=codes[:, first:last].bitcast(fmt), scales=plane[:, first:last], in_=grouped)
+
+        interleave(nc.scalar.copy, g_bf[0], g_raw[0], 0, HALF)
+        quantise(E5M2, g_codes, g_plane, g_bf[0][:], 0, HALF)
+        interleave(nc.scalar.copy, g_bf[1], g_raw[1], G_VECTOR, HALF)
+        interleave(nc.vector.tensor_copy, g_bf[1], g_raw[1], 0, G_VECTOR)
+        deal_words(nc, wd_codes[:], wd_raw[:])
+        quantise(E5M2, g_codes, g_plane, g_bf[1][:], HALF, T)
+        for j in range(PACK):
+            first_pass(j, wd_codes, wd_plane[:, 0, :], g_codes[:].bitcast(E5M2), g_plane[:], False, True)
+        nc.vector.tensor_copy(
+            out=wu_codes[:].rearrange("p (j m e) -> p j m e", j=PACK, e=2),
+            in_=wu_raw[:].rearrange("p (m j e) -> p j m e", j=PACK, e=2),
+        )
+        nc.gpsimd.tensor_scalar(out=us_half[:], in0=us_raw[:], scalar1=0.5, scalar2=0.0, op0=ALU.mult, op1=ALU.add)
+        nc.gpsimd.tensor_scalar(out=us_eighth[:], in0=us_raw[:], scalar1=0.125, scalar2=0.0, op0=ALU.mult, op1=ALU.add)
+
+        groups = T // GROUP
+        own = sb.tile([P, groups, PACK, GROUP], F32, align_bytes=64)
+        sums = [sb.tile([P, groups], F32, name="sums%d" % j, align_bytes=64) for j in range(PACK)]
+        shared = sb.tile([P, PACK, groups], F32, align_bytes=64)
+
+        def take_own(j):
+            nc.scalar.activation(
+                out=own[:, :, j, :], in_=d_banks[j][:].rearrange("p (b i) -> p b i", i=GROUP),
+                func=ACT.Copy, scale=us_half[:, j : j + 1],
+            )
+
+        def take_sums(j):
+            nc.vector.tensor_reduce(
+                out=sums[j][:], in_=d_banks[j][:].rearrange("p (b i) -> p b i", i=GROUP), axis=AXIS.X, op=ALU.add
+            )
+
+        def scale_sums(engine, j):
+            engine.tensor_scalar(
+                out=shared[:, j, :], in0=sums[j][:], scalar1=us_eighth[:, j : j + 1], scalar2=0.0, op0=ALU.mult, op1=ALU.add
+            )
+
+        take_own(1)
+        for j in (0, 2, 3):
+            take_sums(j)
+            scale_sums(nc.gpsimd, j)
+            take_own(j)
+        take_sums(1)
+        deal_scales(nc, wu_plane[:], wu_plane_raw[:])
+        scale_sums(nc.vector, 1)
+
+        for w in range(WARM):
+            spare = ps.tile([P, T], F32, name="spare%d" % w, tag="d%d" % (0, 2, 1, 3)[w % PACK])
+            nc.tensor.matmul_mx(
+                out=spare[:], lhsT=ws_codes[0][:, 0:P].bitcast(E4M3), lhsT_scale=ws_plane[:, 0, 0:P],
+                rhs=xq_codes[:, 0, :].bitcast(E2M1), rhs_scale=xq_plane[:, 0, :], start=True, stop=True,
+            )
+
+        dz_bf = [sb.tile([P, PACK * HALF], BF16, name="dz_bf%d" % h, align_bytes=64) for h in range(2)]
+        dz_codes = sb.tile([P, T], I32, align_bytes=64)
+        dz_plane = sb.tile([P, T], U8, align_bytes=64)
+        half_groups = groups // 2
+        for h in range(2):
+            bs = slice(h * half_groups, (h + 1) * half_groups)
+            nc.vector.tensor_tensor(
+                out=dz_bf[h][:].rearrange("p (b i j) -> p b j i", i=GROUP, j=PACK),
+                in0=own[:, bs, :, :],
+                in1=shared[:, :, bs].rearrange("p j b -> p b j").unsqueeze(3).to_broadcast([P, half_groups, PACK, GROUP]),
+                op=ALU.add,
+            )
+        for h in range(2):
+            quantise(E5M2, dz_codes, dz_plane, dz_bf[h][:], h * HALF, (h + 1) * HALF)
+
+        y = sb.tile([P, PACK, T], F32, align_bytes=64)
+        out_rows = out_0.rearrange("(p j) t -> p j t", j=PACK)
+        for j in range(PACK):
+            y_bank = ps.tile([P, T], F32, name="y_bank%d" % j, tag="y%d" % j)
+            nc.tensor.matmul_mx(
+                out=y_bank[:], lhsT=wu_codes[:, 2 * P * j : 2 * P * (j + 1)].bitcast(E2M1),
+                lhsT_scale=wu_plane[:, 0, j * P : (j + 1) * P],
+                rhs=dz_codes[:].bitcast(E5M2), rhs_scale=dz_plane[:], start=True, stop=True,
+            )
+            copy = nc.scalar.copy if j % 2 == 0 else nc.vector.tensor_copy
+            copy(out=y[:, j, :], in_=y_bank[:])
+            nc.sync.dma_start(out=out_rows[:, j, :], in_=y[:, j, :])
+
+        y_bf = sb.tile([P, PACK * T], BF16, align_bytes=64)
+        y_codes = sb.tile([P, T], I32, align_bytes=64)
+        y_plane = sb.tile([P, T], U8, align_bytes=64)
+        interleave(nc.scalar.copy, y_bf, y, Y_VECTOR, T)
+        interleave(nc.vector.tensor_copy, y_bf, y, 0, Y_VECTOR)
+        quantise(E4M3, y_codes, y_plane, y_bf[:], 0, T)
+        nc.sync.dma_start(out=out_1[0].rearrange("p c t -> p (c t)").bitcast(I32), in_=y_codes[:])
+        for q in range(4):
+            queue = nc.scalar if q % 2 == 0 else nc.sync
+            queue.dma_start(
+                out=out_2[0, 4 * q : 4 * q + 4, :].bitcast(I32), in_=y_plane[32 * q : 32 * q + 4, :].bitcast(I32)
+            )

@@ -21,8 +21,9 @@ PACK = 4
 GROUP = 4
 HALF = T // 2
 G_VECTOR = 168
-Y_VECTOR = 336
-WARM = 0
+Y_VECTOR = (160, 96)
+WARM = 11
+WARM_HEAD = 3
 
 
 def load_scale_rows(queue, plane, scales, quadrant):
@@ -86,8 +87,8 @@ def tile_mix_gradient_shared_by_neighbours_pl_kernel(
         warm = sb.tile([P, 1], F32, align_bytes=64)
         warm_out = sb.tile([P, 1], F32, align_bytes=64)
 
-        nc.gpsimd.memset(ws_plane_raw[:].bitcast(I32), 0)
-        for plane in (xq_plane, wd_plane_raw, wu_plane_raw):
+        nc.gpsimd.memset(wd_plane_raw[:].bitcast(I32), 0)
+        for plane in (ws_plane_raw, xq_plane, wu_plane_raw):
             nc.vector.memset(plane[:].bitcast(I32), 0)
         nc.vector.memset(warm[:], 0.0)
         nc.scalar.activation(out=warm_out[:], in_=warm[:], func=ACT.Copy)
@@ -96,19 +97,17 @@ def tile_mix_gradient_shared_by_neighbours_pl_kernel(
         nc.sync.dma_start(out=ws_raw[0][:], in_=ws_words[0].rearrange("p c t -> p (c t)").bitcast(I32))
         for q in range(4):
             load_scale_rows(nc.sync, ws_plane_raw, ws_scales, q)
-        for q in range(2):
-            load_scale_rows(nc.sync, xq_plane, xq_scales, q)
         nc.sync.dma_start(out=xq_codes[:].bitcast(I32), in_=xq_words.rearrange("z p c -> p z c").bitcast(I32))
-        for q in range(2, 4):
-            load_scale_rows(nc.sync, xq_plane, xq_scales, q)
         nc.sync.dma_start(out=ws_raw[1][:], in_=ws_words[1].rearrange("p c t -> p (c t)").bitcast(I32))
         nc.sync.dma_start(out=g_raw[0][:], in_=g_rows[:, :, 0:HALF])
         for q in range(4):
-            load_scale_rows(nc.sync, wd_plane_raw, wd_scales, q)
+            load_scale_rows(nc.sync, xq_plane, xq_scales, q)
         nc.sync.dma_start(out=g_raw[1][:], in_=g_rows[:, :, HALF:T])
         nc.sync.dma_start(out=wd_raw[:], in_=wd_words[0].rearrange("p c t -> p (c t)").bitcast(I32))
-        nc.sync.dma_start(out=wu_raw[:].bitcast(I32), in_=wu_words[0].bitcast(I32))
+        for q in range(4):
+            load_scale_rows(nc.gpsimd if q < 2 else nc.sync, wd_plane_raw, wd_scales, q)
         nc.sync.dma_start(out=us_raw[:], in_=us.rearrange("(p j) o -> p (j o)", j=PACK))
+        nc.sync.dma_start(out=wu_raw[:].bitcast(I32), in_=wu_words[0].bitcast(I32))
         for q in range(4):
             load_scale_rows(nc.sync, wu_plane_raw, wu_scales, q)
 
@@ -121,22 +120,33 @@ def tile_mix_gradient_shared_by_neighbours_pl_kernel(
                 rhs=moving, rhs_scale=moving_plane, start=start, stop=stop,
             )
 
+        def keep_warm(name, tag):
+            spare = ps.tile([P, T], F32, name=name, tag=tag)
+            nc.tensor.matmul_mx(
+                out=spare[:], lhsT=ws_raw[0][:, 0:P].bitcast(E4M3), lhsT_scale=ws_plane_raw[:, 0, 0:P],
+                rhs=xq_codes[:, 0, :].bitcast(E2M1), rhs_scale=ws_plane_raw[:, 0, :], start=True, stop=True,
+            )
+
+        for w in range(WARM_HEAD):
+            keep_warm("early%d" % w, "y%d" % w)
+        deal_words(nc, ws_codes[0][:], ws_raw[0][:])
         deal_scales(nc, ws_plane[:], ws_plane_raw[:])
+        deal_words(nc, ws_codes[1][:], ws_raw[1][:])
         for z in range(2):
-            deal_words(nc, ws_codes[z][:], ws_raw[z][:])
             for j in range(PACK):
                 first_pass(j, ws_codes[z], ws_plane[:, z, :], xq_codes[:, z, :].bitcast(E2M1), xq_plane[:, z, :], z == 0, False)
-        deal_scales(nc, wd_plane[:], wd_plane_raw[:])
 
         def quantise(fmt, codes, plane, grouped, first, last):
             nc.vector.quantize_mx(out=codes[:, first:last].bitcast(fmt), scales=plane[:, first:last], in_=grouped)
 
-        interleave(nc.scalar.copy, g_bf[0], g_raw[0], 0, HALF)
+        interleave(nc.scalar.copy, g_bf[0], g_raw[0], G_VECTOR, HALF)
+        interleave(nc.vector.tensor_copy, g_bf[0], g_raw[0], 0, G_VECTOR)
         quantise(E5M2, g_codes, g_plane, g_bf[0][:], 0, HALF)
         interleave(nc.scalar.copy, g_bf[1], g_raw[1], G_VECTOR, HALF)
         interleave(nc.vector.tensor_copy, g_bf[1], g_raw[1], 0, G_VECTOR)
         deal_words(nc, wd_codes[:], wd_raw[:])
         quantise(E5M2, g_codes, g_plane, g_bf[1][:], HALF, T)
+        deal_scales(nc, wd_plane[:], wd_plane_raw[:])
         for j in range(PACK):
             first_pass(j, wd_codes, wd_plane[:, 0, :], g_codes[:].bitcast(E5M2), g_plane[:], False, True)
         nc.vector.tensor_copy(
@@ -177,11 +187,7 @@ def tile_mix_gradient_shared_by_neighbours_pl_kernel(
         scale_sums(nc.vector, 1)
 
         for w in range(WARM):
-            spare = ps.tile([P, T], F32, name="spare%d" % w, tag="d%d" % (0, 2, 1, 3)[w % PACK])
-            nc.tensor.matmul_mx(
-                out=spare[:], lhsT=ws_codes[0][:, 0:P].bitcast(E4M3), lhsT_scale=ws_plane[:, 0, 0:P],
-                rhs=xq_codes[:, 0, :].bitcast(E2M1), rhs_scale=xq_plane[:, 0, :], start=True, stop=True,
-            )
+            keep_warm("spare%d" % w, "d%d" % (0, 2, 1, 3)[w % PACK])
 
         dz_bf = [sb.tile([P, PACK * HALF], BF16, name="dz_bf%d" % h, align_bytes=64) for h in range(2)]
         dz_codes = sb.tile([P, T], I32, align_bytes=64)
@@ -200,6 +206,7 @@ def tile_mix_gradient_shared_by_neighbours_pl_kernel(
 
         y = sb.tile([P, PACK, T], F32, align_bytes=64)
         out_rows = out_0.rearrange("(p j) t -> p j t", j=PACK)
+        halves = (slice(0, HALF), slice(HALF, T))
         for j in range(PACK):
             y_bank = ps.tile([P, T], F32, name="y_bank%d" % j, tag="y%d" % j)
             nc.tensor.matmul_mx(
@@ -208,16 +215,23 @@ def tile_mix_gradient_shared_by_neighbours_pl_kernel(
                 rhs=dz_codes[:].bitcast(E5M2), rhs_scale=dz_plane[:], start=True, stop=True,
             )
             copy = nc.scalar.copy if j % 2 == 0 else nc.vector.tensor_copy
-            copy(out=y[:, j, :], in_=y_bank[:])
-            nc.sync.dma_start(out=out_rows[:, j, :], in_=y[:, j, :])
+            for cols in halves if j in (0, PACK - 1) else (slice(0, T),):
+                copy(out=y[:, j, cols], in_=y_bank[:, cols])
+                if j == 0:
+                    nc.sync.dma_start(out=out_rows[:, j, cols], in_=y[:, j, cols])
+            if j > 0:
+                nc.sync.dma_start(out=out_rows[:, j, :], in_=y[:, j, :])
 
-        y_bf = sb.tile([P, PACK * T], BF16, align_bytes=64)
+        y_bf = [sb.tile([P, PACK * HALF], BF16, name="y_bf%d" % h, align_bytes=64) for h in range(2)]
         y_codes = sb.tile([P, T], I32, align_bytes=64)
         y_plane = sb.tile([P, T], U8, align_bytes=64)
-        interleave(nc.scalar.copy, y_bf, y, Y_VECTOR, T)
-        interleave(nc.vector.tensor_copy, y_bf, y, 0, Y_VECTOR)
-        quantise(E4M3, y_codes, y_plane, y_bf[:], 0, T)
-        nc.sync.dma_start(out=out_1[0].rearrange("p c t -> p (c t)").bitcast(I32), in_=y_codes[:])
+        for h in range(2):
+            interleave(nc.scalar.copy, y_bf[h], y[:, :, halves[h]], Y_VECTOR[h], HALF)
+            interleave(nc.vector.tensor_copy, y_bf[h], y[:, :, halves[h]], 0, Y_VECTOR[h])
+        words_out = out_1[0].rearrange("p c t -> p (c t)").bitcast(I32)
+        for h in range(2):
+            quantise(E4M3, y_codes, y_plane, y_bf[h][:], h * HALF, (h + 1) * HALF)
+            nc.sync.dma_start(out=words_out[:, halves[h]], in_=y_codes[:, halves[h]])
         for q in range(4):
             queue = nc.scalar if q % 2 == 0 else nc.sync
             queue.dma_start(

@@ -21,8 +21,9 @@ PACK = 4
 GROUP = 4
 HALF = T // 2
 G_VECTOR = 168
-Y_VECTOR = (160, 96)
-WARM = 11
+Y_VECTOR = 168
+QUARTER = T // 4
+WARM = 8
 WARM_HEAD = 3
 
 
@@ -79,8 +80,8 @@ def tile_mix_gradient_shared_by_neighbours_pl_kernel(
         wu_codes = sb.tile([P, 2 * K], U8, align_bytes=64)
         g_raw = [sb.tile([P, PACK, HALF], F32, name="g_raw%d" % h, align_bytes=64) for h in range(2)]
         g_bf = [sb.tile([P, PACK * HALF], BF16, name="g_bf%d" % h, align_bytes=64) for h in range(2)]
-        g_codes = sb.tile([P, T], I32, align_bytes=64)
-        g_plane = sb.tile([P, T], U8, align_bytes=64)
+        e5_codes = sb.tile([P, 2 * T], I32, align_bytes=64)
+        e5_plane = sb.tile([P, 2 * T], U8, align_bytes=64)
         us_raw = sb.tile([P, PACK], F32, align_bytes=64)
         us_half = sb.tile([P, PACK], F32, align_bytes=64)
         us_eighth = sb.tile([P, PACK], F32, align_bytes=64)
@@ -141,20 +142,20 @@ def tile_mix_gradient_shared_by_neighbours_pl_kernel(
 
         interleave(nc.scalar.copy, g_bf[0], g_raw[0], G_VECTOR, HALF)
         interleave(nc.vector.tensor_copy, g_bf[0], g_raw[0], 0, G_VECTOR)
-        quantise(E5M2, g_codes, g_plane, g_bf[0][:], 0, HALF)
+        quantise(E5M2, e5_codes, e5_plane, g_bf[0][:], 0, HALF)
         interleave(nc.scalar.copy, g_bf[1], g_raw[1], G_VECTOR, HALF)
         interleave(nc.vector.tensor_copy, g_bf[1], g_raw[1], 0, G_VECTOR)
         deal_words(nc, wd_codes[:], wd_raw[:])
-        quantise(E5M2, g_codes, g_plane, g_bf[1][:], HALF, T)
+        quantise(E5M2, e5_codes, e5_plane, g_bf[1][:], HALF, T)
         deal_scales(nc, wd_plane[:], wd_plane_raw[:])
         for j in range(PACK):
-            first_pass(j, wd_codes, wd_plane[:, 0, :], g_codes[:].bitcast(E5M2), g_plane[:], False, True)
+            first_pass(j, wd_codes, wd_plane[:, 0, :], e5_codes[:, 0:T].bitcast(E5M2), e5_plane[:, 0:T], False, True)
         nc.vector.tensor_copy(
             out=wu_codes[:].rearrange("p (j m e) -> p j m e", j=PACK, e=2),
             in_=wu_raw[:].rearrange("p (m j e) -> p j m e", j=PACK, e=2),
         )
-        nc.gpsimd.tensor_scalar(out=us_half[:], in0=us_raw[:], scalar1=0.5, scalar2=0.0, op0=ALU.mult, op1=ALU.add)
-        nc.gpsimd.tensor_scalar(out=us_eighth[:], in0=us_raw[:], scalar1=0.125, scalar2=0.0, op0=ALU.mult, op1=ALU.add)
+        nc.scalar.activation(out=us_eighth[:], in_=us_raw[:], func=ACT.Copy, scale=0.125)
+        nc.scalar.activation(out=us_half[:], in_=us_raw[:], func=ACT.Copy, scale=0.5)
 
         groups = T // GROUP
         own = sb.tile([P, groups, PACK, GROUP], F32, align_bytes=64)
@@ -190,48 +191,79 @@ def tile_mix_gradient_shared_by_neighbours_pl_kernel(
             keep_warm("spare%d" % w, "d%d" % (0, 2, 1, 3)[w % PACK])
 
         dz_bf = [sb.tile([P, PACK * HALF], BF16, name="dz_bf%d" % h, align_bytes=64) for h in range(2)]
-        dz_codes = sb.tile([P, T], I32, align_bytes=64)
-        dz_plane = sb.tile([P, T], U8, align_bytes=64)
-        half_groups = groups // 2
-        for h in range(2):
-            bs = slice(h * half_groups, (h + 1) * half_groups)
-            nc.vector.tensor_tensor(
-                out=dz_bf[h][:].rearrange("p (b i j) -> p b j i", i=GROUP, j=PACK),
-                in0=own[:, bs, :, :],
-                in1=shared[:, :, bs].rearrange("p j b -> p b j").unsqueeze(3).to_broadcast([P, half_groups, PACK, GROUP]),
-                op=ALU.add,
-            )
-        for h in range(2):
-            quantise(E5M2, dz_codes, dz_plane, dz_bf[h][:], h * HALF, (h + 1) * HALF)
-
-        y = sb.tile([P, PACK, T], F32, align_bytes=64)
-        out_rows = out_0.rearrange("(p j) t -> p j t", j=PACK)
-        halves = (slice(0, HALF), slice(HALF, T))
-        for j in range(PACK):
-            y_bank = ps.tile([P, T], F32, name="y_bank%d" % j, tag="y%d" % j)
-            nc.tensor.matmul_mx(
-                out=y_bank[:], lhsT=wu_codes[:, 2 * P * j : 2 * P * (j + 1)].bitcast(E2M1),
-                lhsT_scale=wu_plane[:, 0, j * P : (j + 1) * P],
-                rhs=dz_codes[:].bitcast(E5M2), rhs_scale=dz_plane[:], start=True, stop=True,
-            )
-            copy = nc.scalar.copy if j % 2 == 0 else nc.vector.tensor_copy
-            for cols in halves if j in (0, PACK - 1) else (slice(0, T),):
-                copy(out=y[:, j, cols], in_=y_bank[:, cols])
-                if j == 0:
-                    nc.sync.dma_start(out=out_rows[:, j, cols], in_=y[:, j, cols])
-            if j > 0:
-                nc.sync.dma_start(out=out_rows[:, j, :], in_=y[:, j, :])
-
+        y = [sb.tile([P, PACK, HALF], F32, name="y%d" % h, align_bytes=64) for h in range(2)]
         y_bf = [sb.tile([P, PACK * HALF], BF16, name="y_bf%d" % h, align_bytes=64) for h in range(2)]
         y_codes = sb.tile([P, T], I32, align_bytes=64)
         y_plane = sb.tile([P, T], U8, align_bytes=64)
-        for h in range(2):
-            interleave(nc.scalar.copy, y_bf[h], y[:, :, halves[h]], Y_VECTOR[h], HALF)
-            interleave(nc.vector.tensor_copy, y_bf[h], y[:, :, halves[h]], 0, Y_VECTOR[h])
+        out_rows = out_0.rearrange("(p j) t -> p j t", j=PACK)
         words_out = out_1[0].rearrange("p c t -> p (c t)").bitcast(I32)
-        for h in range(2):
-            quantise(E4M3, y_codes, y_plane, y_bf[h][:], h * HALF, (h + 1) * HALF)
-            nc.sync.dma_start(out=words_out[:, halves[h]], in_=y_codes[:, halves[h]])
+
+        def blend(first, last):
+            h = first // HALF
+            bs = slice(first // GROUP, last // GROUP)
+            nc.vector.tensor_tensor(
+                out=dz_bf[h][:, PACK * (first - h * HALF) : PACK * (last - h * HALF)].rearrange(
+                    "p (b i j) -> p b j i", i=GROUP, j=PACK
+                ),
+                in0=own[:, bs, :, :],
+                in1=shared[:, :, bs].rearrange("p j b -> p b j").unsqueeze(3).to_broadcast(
+                    [P, (last - first) // GROUP, PACK, GROUP]
+                ),
+                op=ALU.add,
+            )
+
+        def quantise_dz(first, last):
+            h = first // HALF
+            grouped = dz_bf[h][:, PACK * (first - h * HALF) : PACK * (last - h * HALF)]
+            quantise(E5M2, e5_codes, e5_plane, grouped, T + first, T + last)
+
+        def second_passes(h, tag):
+            window = slice((h + 1) * HALF, (h + 1) * HALF + T)
+            banks = [ps.tile([P, T], F32, name="y_bank%d%d" % (h, j), tag="%s%d" % (tag, j)) for j in range(PACK)]
+            for j in range(PACK):
+                nc.tensor.matmul_mx(
+                    out=banks[j][:], lhsT=wu_codes[:, 2 * P * j : 2 * P * (j + 1)].bitcast(E2M1),
+                    lhsT_scale=wu_plane[:, 0, j * P : (j + 1) * P],
+                    rhs=e5_codes[:, window].bitcast(E5M2), rhs_scale=e5_plane[:, window], start=True, stop=True,
+                )
+            return banks
+
+        def take_out(copy, banks, h, j):
+            copy(out=y[h][:, j, :], in_=banks[j][:, HALF:T])
+            if j % 2 == 1:
+                nc.sync.dma_start(
+                    out=out_rows[:, j - 1 : j + 1, h * HALF : (h + 1) * HALF], in_=y[h][:, j - 1 : j + 1, :]
+                )
+
+        def quantise_y(first, last):
+            h = first // HALF
+            grouped = y_bf[h][:, PACK * (first - h * HALF) : PACK * (last - h * HALF)]
+            quantise(E4M3, y_codes, y_plane, grouped, first, last)
+
+        def store_words(h):
+            nc.sync.dma_start(out=words_out[:, h * HALF : (h + 1) * HALF], in_=y_codes[:, h * HALF : (h + 1) * HALF])
+
+        blend(0, HALF)
+        blend(HALF, HALF + QUARTER)
+        quantise_dz(0, HALF)
+        banks = second_passes(0, "y")
+        for j in range(PACK):
+            take_out(nc.scalar.copy, banks, 0, j)
+        blend(HALF + QUARTER, T)
+        quantise_dz(HALF, HALF + QUARTER)
+        quantise_dz(HALF + QUARTER, T)
+        banks = second_passes(1, "d")
+        for j in range(PACK):
+            take_out(nc.scalar.copy, banks, 1, j)
+        interleave(nc.vector.tensor_copy, y_bf[0], y[0], 0, HALF)
+        quantise_y(0, HALF)
+        store_words(0)
+        interleave(nc.scalar.copy, y_bf[1], y[1], Y_VECTOR, HALF)
+        interleave(nc.vector.tensor_copy, y_bf[1], y[1], 0, QUARTER)
+        interleave(nc.vector.tensor_copy, y_bf[1], y[1], QUARTER, Y_VECTOR)
+        quantise_y(HALF, HALF + QUARTER)
+        quantise_y(HALF + QUARTER, T)
+        store_words(1)
         for q in range(4):
             queue = nc.scalar if q % 2 == 0 else nc.sync
             queue.dma_start(

from contextlib import ExitStack

import concourse.mybir as mybir

N, L, R, K, T = 512, 1024, 512, 512, 512
FLOPS = 2 * T * (N * R + L * R + R * K)

F32 = mybir.dt.float32
BF16 = mybir.dt.bfloat16
I32 = mybir.dt.int32
U8 = mybir.dt.uint8
E4M3 = mybir.dt.float8_e4m3fn_x4
E5M2 = mybir.dt.float8_e5m2_x4
E2M1 = mybir.dt.float4_e2m1fn_x4
ALU = mybir.AluOpType
ACT = mybir.ActivationFunctionType
AXIS = mybir.AxisListType

P = 128
PACK = 4
GROUP = 4
HALF = T // 2
G_VECTOR = 168
Y_VECTOR = 168
QUARTER = T // 4
WARM = 8
WARM_HEAD = 3


def load_scale_rows(queue, plane, scales, quadrant):
    queue.dma_start(
        out=plane[32 * quadrant : 32 * quadrant + 4, :, :].bitcast(I32),
        in_=scales[:, 4 * quadrant : 4 * quadrant + 4, :].rearrange("z r c -> r z c").bitcast(I32),
    )


def deal_words(nc, dealt, raw):
    nc.vector.tensor_copy(
        out=dealt.rearrange("p (j c i) -> p c j i", j=PACK, i=4),
        in_=raw.rearrange("p (c i j) -> p c j i", j=PACK, i=4),
    )


def deal_scales(nc, dealt, raw):
    nc.vector.tensor_copy(
        out=dealt.rearrange("p z (j m) -> p z j m", j=PACK),
        in_=raw.rearrange("p z (m j) -> p z j m", j=PACK),
    )


def interleave(copy, grouped, rows, first, last):
    copy(
        out=grouped[:, PACK * first : PACK * last].rearrange("p (c i j) -> p c j i", i=4, j=PACK),
        in_=rows[:, :, first:last].rearrange("p j (c i) -> p c j i", i=4),
    )


def tile_mix_gradient_shared_by_neighbours_pl_kernel(
    tc, g, wd_words, wd_scales, xq_words, xq_scales, ws_words, ws_scales, us, wu_words, wu_scales, out_0, out_1, out_2
):
    nc = tc.nc
    with ExitStack() as ctx:
        sb = ctx.enter_context(tc.tile_pool(name="sb", bufs=1))
        ps = ctx.enter_context(tc.psum_pool(name="ps", bufs=1))
        ctx.enter_context(tc.manual_schedule())

        ws_plane_raw = sb.tile([P, 2, R], U8, align_bytes=64)
        xq_plane = sb.tile([P, 2, T], U8, align_bytes=64)
        wd_plane_raw = sb.tile([P, 1, R], U8, align_bytes=64)
        wu_plane_raw = sb.tile([P, 1, K], U8, align_bytes=64)
        ws_plane = sb.tile([P, 2, R], U8, align_bytes=64)
        wd_plane = sb.tile([P, 1, R], U8, align_bytes=64)
        wu_plane = sb.tile([P, 1, K], U8, align_bytes=64)
        ws_raw = [sb.tile([P, R], I32, name="ws_raw%d" % z, align_bytes=64) for z in range(2)]
        ws_codes = [sb.tile([P, R], I32, name="ws_codes%d" % z, align_bytes=64) for z in range(2)]
        wd_raw = sb.tile([P, R], I32, align_bytes=64)
        wd_codes = sb.tile([P, R], I32, align_bytes=64)
        xq_codes = sb.tile([P, 2, 2 * T], U8, align_bytes=64)
        wu_raw = sb.tile([P, 2 * K], U8, align_bytes=64)
        wu_codes = sb.tile([P, 2 * K], U8, align_bytes=64)
        g_raw = [sb.tile([P, PACK, HALF], F32, name="g_raw%d" % h, align_bytes=64) for h in range(2)]
        g_bf = [sb.tile([P, PACK * HALF], BF16, name="g_bf%d" % h, align_bytes=64) for h in range(2)]
        e5_codes = sb.tile([P, 2 * T], I32, align_bytes=64)
        e5_plane = sb.tile([P, 2 * T], U8, align_bytes=64)
        us_raw = sb.tile([P, PACK], F32, align_bytes=64)
        us_half = sb.tile([P, PACK], F32, align_bytes=64)
        us_eighth = sb.tile([P, PACK], F32, align_bytes=64)
        warm = sb.tile([P, 1], F32, align_bytes=64)
        warm_out = sb.tile([P, 1], F32, align_bytes=64)

        nc.gpsimd.memset(wd_plane_raw[:].bitcast(I32), 0)
        for plane in (ws_plane_raw, xq_plane, wu_plane_raw):
            nc.vector.memset(plane[:].bitcast(I32), 0)
        nc.vector.memset(warm[:], 0.0)
        nc.scalar.activation(out=warm_out[:], in_=warm[:], func=ACT.Copy)

        g_rows = g.rearrange("(p j) t -> p j t", j=PACK)
        nc.sync.dma_start(out=ws_raw[0][:], in_=ws_words[0].rearrange("p c t -> p (c t)").bitcast(I32))
        for q in range(4):
            load_scale_rows(nc.sync, ws_plane_raw, ws_scales, q)
        nc.sync.dma_start(out=xq_codes[:].bitcast(I32), in_=xq_words.rearrange("z p c -> p z c").bitcast(I32))
        nc.sync.dma_start(out=ws_raw[1][:], in_=ws_words[1].rearrange("p c t -> p (c t)").bitcast(I32))
        nc.sync.dma_start(out=g_raw[0][:], in_=g_rows[:, :, 0:HALF])
        for q in range(4):
            load_scale_rows(nc.sync, xq_plane, xq_scales, q)
        nc.sync.dma_start(out=g_raw[1][:], in_=g_rows[:, :, HALF:T])
        nc.sync.dma_start(out=wd_raw[:], in_=wd_words[0].rearrange("p c t -> p (c t)").bitcast(I32))
        for q in range(4):
            load_scale_rows(nc.gpsimd if q < 2 else nc.sync, wd_plane_raw, wd_scales, q)
        nc.sync.dma_start(out=us_raw[:], in_=us.rearrange("(p j) o -> p (j o)", j=PACK))
        nc.sync.dma_start(out=wu_raw[:].bitcast(I32), in_=wu_words[0].bitcast(I32))
        for q in range(4):
            load_scale_rows(nc.sync, wu_plane_raw, wu_scales, q)

        d_banks = [ps.tile([P, T], F32, name="d_bank%d" % j, tag="d%d" % j) for j in range(PACK)]

        def first_pass(j, codes, plane, moving, moving_plane, start, stop):
            cols = slice(j * P, (j + 1) * P)
            nc.tensor.matmul_mx(
                out=d_banks[j][:], lhsT=codes[:, cols].bitcast(E4M3), lhsT_scale=plane[:, cols],
                rhs=moving, rhs_scale=moving_plane, start=start, stop=stop,
            )

        def keep_warm(name, tag):
            spare = ps.tile([P, T], F32, name=name, tag=tag)
            nc.tensor.matmul_mx(
                out=spare[:], lhsT=ws_raw[0][:, 0:P].bitcast(E4M3), lhsT_scale=ws_plane_raw[:, 0, 0:P],
                rhs=xq_codes[:, 0, :].bitcast(E2M1), rhs_scale=ws_plane_raw[:, 0, :], start=True, stop=True,
            )

        for w in range(WARM_HEAD):
            keep_warm("early%d" % w, "y%d" % w)
        deal_words(nc, ws_codes[0][:], ws_raw[0][:])
        deal_scales(nc, ws_plane[:], ws_plane_raw[:])
        deal_words(nc, ws_codes[1][:], ws_raw[1][:])
        for z in range(2):
            for j in range(PACK):
                first_pass(j, ws_codes[z], ws_plane[:, z, :], xq_codes[:, z, :].bitcast(E2M1), xq_plane[:, z, :], z == 0, False)

        def quantise(fmt, codes, plane, grouped, first, last):
            nc.vector.quantize_mx(out=codes[:, first:last].bitcast(fmt), scales=plane[:, first:last], in_=grouped)

        interleave(nc.scalar.copy, g_bf[0], g_raw[0], G_VECTOR, HALF)
        interleave(nc.vector.tensor_copy, g_bf[0], g_raw[0], 0, G_VECTOR)
        quantise(E5M2, e5_codes, e5_plane, g_bf[0][:], 0, HALF)
        interleave(nc.scalar.copy, g_bf[1], g_raw[1], G_VECTOR, HALF)
        interleave(nc.vector.tensor_copy, g_bf[1], g_raw[1], 0, G_VECTOR)
        deal_words(nc, wd_codes[:], wd_raw[:])
        quantise(E5M2, e5_codes, e5_plane, g_bf[1][:], HALF, T)
        deal_scales(nc, wd_plane[:], wd_plane_raw[:])
        for j in range(PACK):
            first_pass(j, wd_codes, wd_plane[:, 0, :], e5_codes[:, 0:T].bitcast(E5M2), e5_plane[:, 0:T], False, True)
        nc.vector.tensor_copy(
            out=wu_codes[:].rearrange("p (j m e) -> p j m e", j=PACK, e=2),
            in_=wu_raw[:].rearrange("p (m j e) -> p j m e", j=PACK, e=2),
        )
        nc.scalar.activation(out=us_eighth[:], in_=us_raw[:], func=ACT.Copy, scale=0.125)
        nc.scalar.activation(out=us_half[:], in_=us_raw[:], func=ACT.Copy, scale=0.5)

        groups = T // GROUP
        own = sb.tile([P, groups, PACK, GROUP], F32, align_bytes=64)
        sums = [sb.tile([P, groups], F32, name="sums%d" % j, align_bytes=64) for j in range(PACK)]
        shared = sb.tile([P, PACK, groups], F32, align_bytes=64)

        def take_own(j):
            nc.scalar.activation(
                out=own[:, :, j, :], in_=d_banks[j][:].rearrange("p (b i) -> p b i", i=GROUP),
                func=ACT.Copy, scale=us_half[:, j : j + 1],
            )

        def take_sums(j):
            nc.vector.tensor_reduce(
                out=sums[j][:], in_=d_banks[j][:].rearrange("p (b i) -> p b i", i=GROUP), axis=AXIS.X, op=ALU.add
            )

        def scale_sums(engine, j):
            engine.tensor_scalar(
                out=shared[:, j, :], in0=sums[j][:], scalar1=us_eighth[:, j : j + 1], scalar2=0.0, op0=ALU.mult, op1=ALU.add
            )

        take_own(1)
        for j in (0, 2, 3):
            take_sums(j)
            scale_sums(nc.gpsimd, j)
            take_own(j)
        take_sums(1)
        deal_scales(nc, wu_plane[:], wu_plane_raw[:])
        scale_sums(nc.vector, 1)

        for w in range(WARM):
            keep_warm("spare%d" % w, "d%d" % (0, 2, 1, 3)[w % PACK])

        dz_bf = [sb.tile([P, PACK * HALF], BF16, name="dz_bf%d" % h, align_bytes=64) for h in range(2)]
        y = [sb.tile([P, PACK, HALF], F32, name="y%d" % h, align_bytes=64) for h in range(2)]
        y_bf = [sb.tile([P, PACK * HALF], BF16, name="y_bf%d" % h, align_bytes=64) for h in range(2)]
        y_codes = sb.tile([P, T], I32, align_bytes=64)
        y_plane = sb.tile([P, T], U8, align_bytes=64)
        out_rows = out_0.rearrange("(p j) t -> p j t", j=PACK)
        words_out = out_1[0].rearrange("p c t -> p (c t)").bitcast(I32)

        def blend(first, last):
            h = first // HALF
            bs = slice(first // GROUP, last // GROUP)
            nc.vector.tensor_tensor(
                out=dz_bf[h][:, PACK * (first - h * HALF) : PACK * (last - h * HALF)].rearrange(
                    "p (b i j) -> p b j i", i=GROUP, j=PACK
                ),
                in0=own[:, bs, :, :],
                in1=shared[:, :, bs].rearrange("p j b -> p b j").unsqueeze(3).to_broadcast(
                    [P, (last - first) // GROUP, PACK, GROUP]
                ),
                op=ALU.add,
            )

        def quantise_dz(first, last):
            h = first // HALF
            grouped = dz_bf[h][:, PACK * (first - h * HALF) : PACK * (last - h * HALF)]
            quantise(E5M2, e5_codes, e5_plane, grouped, T + first, T + last)

        def second_passes(h, tag):
            window = slice((h + 1) * HALF, (h + 1) * HALF + T)
            banks = [ps.tile([P, T], F32, name="y_bank%d%d" % (h, j), tag="%s%d" % (tag, j)) for j in range(PACK)]
            for j in range(PACK):
                nc.tensor.matmul_mx(
                    out=banks[j][:], lhsT=wu_codes[:, 2 * P * j : 2 * P * (j + 1)].bitcast(E2M1),
                    lhsT_scale=wu_plane[:, 0, j * P : (j + 1) * P],
                    rhs=e5_codes[:, window].bitcast(E5M2), rhs_scale=e5_plane[:, window], start=True, stop=True,
                )
            return banks

        def take_out(copy, banks, h, j):
            copy(out=y[h][:, j, :], in_=banks[j][:, HALF:T])
            if j % 2 == 1:
                nc.sync.dma_start(
                    out=out_rows[:, j - 1 : j + 1, h * HALF : (h + 1) * HALF], in_=y[h][:, j - 1 : j + 1, :]
                )

        def quantise_y(first, last):
            h = first // HALF
            grouped = y_bf[h][:, PACK * (first - h * HALF) : PACK * (last - h * HALF)]
            quantise(E4M3, y_codes, y_plane, grouped, first, last)

        def store_words(h):
            nc.sync.dma_start(out=words_out[:, h * HALF : (h + 1) * HALF], in_=y_codes[:, h * HALF : (h + 1) * HALF])

        blend(0, HALF)
        blend(HALF, HALF + QUARTER)
        quantise_dz(0, HALF)
        banks = second_passes(0, "y")
        for j in range(PACK):
            take_out(nc.scalar.copy, banks, 0, j)
        blend(HALF + QUARTER, T)
        quantise_dz(HALF, HALF + QUARTER)
        quantise_dz(HALF + QUARTER, T)
        banks = second_passes(1, "d")
        for j in range(PACK):
            take_out(nc.scalar.copy, banks, 1, j)
        interleave(nc.vector.tensor_copy, y_bf[0], y[0], 0, HALF)
        quantise_y(0, HALF)
        store_words(0)
        interleave(nc.scalar.copy, y_bf[1], y[1], Y_VECTOR, HALF)
        interleave(nc.vector.tensor_copy, y_bf[1], y[1], 0, QUARTER)
        interleave(nc.vector.tensor_copy, y_bf[1], y[1], QUARTER, Y_VECTOR)
        quantise_y(HALF, HALF + QUARTER)
        quantise_y(HALF + QUARTER, T)
        store_words(1)
        for q in range(4):
            queue = nc.scalar if q % 2 == 0 else nc.sync
            queue.dma_start(
                out=out_2[0, 4 * q : 4 * q + 4, :].bitcast(I32), in_=y_plane[32 * q : 32 * q + 4, :].bitcast(I32)
            )
